import numpy as np
import ml_dtypes


def mxq(x, axis, fmt="e4m3"):
    dtype, down = {"e4m3": (ml_dtypes.float8_e4m3fn, 7), "e5m2": (ml_dtypes.float8_e5m2, 14)}[fmt]
    v = np.moveaxis(np.asarray(x, np.float32).astype(ml_dtypes.bfloat16).astype(np.float64), axis, -1)
    blocks = v.reshape(v.shape[:-1] + (-1, 32))
    amax = np.abs(blocks).max(-1, keepdims=True)
    byte = np.maximum(np.where(amax > 0, np.frexp(amax)[1] - 1 + 127, 0) - down, 1)
    scale = np.exp2(byte - 127.0)
    codes = (blocks / scale).astype(np.float32).astype(dtype).astype(np.float64)
    return np.moveaxis((codes * scale).reshape(v.shape), -1, axis)


WIDE = False


def mx_kscale(k):
    if not WIDE:
        return np.ones(k)
    levels = np.array([10, -10, 5, -5, 0])
    if k % 512:
        return np.exp2(np.random.permutation(np.resize(levels, k // 32))).repeat(32)
    a = np.empty((k // 512, 16))
    for p in range(k // 512):
        a[p, :8] = np.random.permutation(np.resize(levels, 8))
        for g in range(8):
            far = levels[np.abs(levels - a[p, g]) >= 10]
            a[p, g + 8] = far[np.random.randint(len(far))]
    return np.exp2(a.ravel()).repeat(32)


def f64(x):
    return np.asarray(x).astype(np.float64)


def striped(idx):
    return np.tile(idx.reshape(-1, 16).T, (8, 1)).astype(np.uint16)


def unstriped(offs):
    return offs[:16].T.reshape(-1).astype(np.int64)


def striped8(idx):
    return np.concatenate([x.reshape(-1, 16).T for x in idx]).astype(np.uint16)


def runs(offs, k):
    lists = np.stack([offs[16 * r : 16 * r + 16].T.reshape(-1) for r in range(8)]).astype(np.int64)
    return lists[np.arange(k) % 512 // 64]


def pack_weight(w):
    k, n = w.shape
    w = f64(np.asarray(w, np.float32).astype(ml_dtypes.bfloat16)).reshape(k // 32, 32, n)
    amax = np.abs(w).max(1)
    byte = np.clip(np.where(amax > 0, np.frexp(amax)[1] - 1 + 127 - 7, 1), 1, 254)
    scaled = (w * np.exp2(127.0 - byte)[:, None, :]).reshape(k, n).astype(np.float32)
    words = np.ascontiguousarray(scaled.reshape(k // 512, 128, 4, n).transpose(0, 1, 3, 2)).astype(ml_dtypes.float8_e4m3fn).view(np.uint8)
    return words, np.ascontiguousarray(byte.astype(np.uint8).reshape(k // 512, 16, n))


def unpack_weight(words, scales):
    g, p, n, _ = words.shape
    vals = np.ascontiguousarray(words).view(ml_dtypes.float8_e4m3fn).astype(np.float64) * np.repeat(np.exp2(scales.astype(np.float64) - 127.0), 8, axis=1)[..., None]
    return vals.transpose(0, 1, 3, 2).reshape(g * 512, n)


K, T, S, N, H = 512, 2048, 512, 512, 512


def setup_inputs():
    n = np.random.standard_normal
    s = mx_kscale(K)[:, None]
    u = mx_kscale(H)
    packed_xT = pack_weight(n((K, T)) * s)
    return {
        "x_words": packed_xT[0],
        "x_scales": packed_xT[1],
        "w1": (n((K, H)) / np.sqrt(K) / s).astype(np.float32),
        "w2": (n((K, H)) / np.sqrt(K) / s).astype(np.float32),
        "gn": (np.random.uniform(0.5, 1.5, (H, 1)) * u[:, None]).astype(np.float32),
        "w3": (n((H, N)) / np.sqrt(H) / u[:, None]).astype(np.float32),
        "res": (2 * n((N, S))).astype(np.float32),
        "offs": striped(np.random.permutation(T)[:S]),
        "two": striped(np.random.permutation(T)[:S]),
        "hi": striped8(np.stack([np.random.permutation(S) for _ in range(8)])),
        "lo": striped8(np.stack([np.random.permutation(S) for _ in range(8)])),
    }


def reference(x_words, x_scales, w1, w2, gn, w3, res, offs, two, hi, lo):
    xq = unpack_weight(x_words, x_scales)[:, unstriped(offs)]
    y = mxq(f64(w1), 0, "e4m3").T @ xq
    dx = y[np.arange(H)[:, None], runs(hi, H)] - (y[np.arange(H)[:, None], runs(lo, H)])
    x_two = unpack_weight(x_words, x_scales)[:, unstriped(two)]
    c = mxq(f64(w2), 0, "e4m3").T @ x_two
    dy = c[np.arange(H)[:, None], runs(hi, H)] - (c[np.arange(H)[:, None], runs(lo, H)])
    z = f64(gn) * ((dx * dy) / ((dx) ** 2 + 0.25))
    return f64(res) + (mxq(f64(w3), 0, "e4m3").T @ mxq(z, 0, "e4m3"))

@@ -1,0 +1,221 @@
+from contextlib import ExitStack
+
+import concourse.mybir as mybir
+
+K, T, S, N, H = 512, 2048, 512, 512, 512
+FLOPS = 2 * K * H * S * 2 + 2 * H * N * S
+
+F32 = mybir.dt.float32
+BF16 = mybir.dt.bfloat16
+I32 = mybir.dt.int32
+U32 = mybir.dt.uint32
+U16 = mybir.dt.uint16
+U8 = mybir.dt.uint8
+FP8X4 = mybir.dt.float8_e4m3fn_x4
+ACT = mybir.ActivationFunctionType
+ALU = mybir.AluOpType
+
+P = 128
+PACK = 4
+LANES = 16
+HALF = S // 2
+CHUNKS = ((0, 256), (256, 128), (384, 128))
+
+
+def tile_picked_localslope_none_p_kernel(
+    tc, x_words, x_scales, w1, w2, gn, w3, res, offs, two, hi, lo, out
+):
+    nc = tc.nc
+
+    with ExitStack() as ctx:
+        lists = ctx.enter_context(tc.tile_pool(name="lists", bufs=1))
+        keep = ctx.enter_context(tc.tile_pool(name="keep", bufs=1))
+        psum = ctx.enter_context(tc.psum_pool(name="psum", bufs=1))
+
+        def load_list(src, name):
+            tile = lists.tile([P, S // LANES], U16, name=name)
+            nc.sync.dma_start(tile[:], src)
+            return tile
+
+        def load_weight_half(w, name, h):
+            rows = w.rearrange("(p j) c -> p j c", j=PACK)
+            raw = keep.tile([P, PACK, H // 2], F32, name=f"{name}_raw{h}")
+            nc.sync.dma_start(raw[:], rows[:, :, h * (H // 2) : (h + 1) * (H // 2)])
+            return raw
+
+        def load_weight_halves(w, name):
+            return [load_weight_half(w, name, h) for h in range(2)]
+
+        def entries(tile, start, count):
+            return tile[:, start // LANES : (start + count) // LANES]
+
+        def bank(b, shape):
+            return psum.tile(shape, F32, name=f"bank{b}", tag=f"bank{b}")
+
+        x_scale_table = keep.tile([P, T], U8, name="x_scale_table")
+        nc.vector.memset(x_scale_table[:].bitcast(I32), 0)
+        scale_rows = x_scales[0].bitcast(I32)
+        offs_t = load_list(offs, "offs_t")
+        two_t = load_list(two, "two_t")
+        w1_raw = [load_weight_half(w1, "w1", 0)]
+        for r in range(PACK):
+            nc.sync.dma_start(x_scale_table[r:P:32, :].bitcast(I32), scale_rows[r:16:PACK, :])
+        w1_raw.append(load_weight_half(w1, "w1", 1))
+        x_word_table = keep.tile([P, T], I32, name="x_word_table")
+        nc.sync.dma_start(x_word_table[:], x_words[0].rearrange("p n t -> p (n t)").bitcast(I32))
+        hi_t = load_list(hi, "hi_t")
+        lo_t = load_list(lo, "lo_t")
+        w2_raw = load_weight_halves(w2, "w2")
+        gain = keep.tile([P, PACK], F32, name="gain")
+        nc.sync.dma_start(gain[:], gn.rearrange("(p t) o -> p (t o)", t=PACK))
+        w3_raw = load_weight_halves(w3, "w3")
+        res_t = keep.tile([P, PACK, S], F32, name="res_t")
+        nc.sync.dma_start(res_t[:], res.rearrange("(b p) j -> p b j", p=P))
+
+        def cast_dealt(halves, name):
+            grouped = keep.tile([P, PACK, P, PACK], BF16, name=name, align_bytes=64)
+            for h, raw in enumerate(halves):
+                nc.scalar.copy(
+                    grouped[:, :, h * 64 : (h + 1) * 64, :].rearrange("p t m j -> p m j t"),
+                    raw[:].rearrange("p j (m t) -> p m j t", t=PACK),
+                )
+            return grouped[:].rearrange("p t m j -> p (t m j)")
+
+        def cast_plain(halves, name):
+            grouped = keep.tile([P, N, PACK], BF16, name=name, align_bytes=64)
+            for h, raw in enumerate(halves):
+                nc.scalar.copy(
+                    grouped[:, h * 256 : (h + 1) * 256, :].rearrange("p (c i) j -> p c j i", i=4),
+                    raw[:].rearrange("p j (c i) -> p c j i", i=4),
+                )
+            return grouped[:].rearrange("p c j -> p (c j)")
+
+        def quantise(values, width, name):
+            words = keep.tile([P, width], U32, name=f"{name}_words", align_bytes=64)
+            scales = keep.tile([P, width], U8, name=f"{name}_scales", align_bytes=64)
+            nc.vector.quantize_mx(out=words[:].bitcast(FP8X4), scales=scales[:], in_=values)
+            return words, scales
+
+        def pick_scales(list_t, name):
+            scales = keep.tile([P, S], U8, name=name, align_bytes=64)
+            nc.vector.tensor_copy(scales[:], x_scale_table[:].indirect(list_t[:]))
+            return scales
+
+        def pick_words(list_t, name):
+            words = keep.tile([P, S], U32, name=name, align_bytes=64)
+            nc.vector.tensor_copy(words[:], x_word_table[:].bitcast(U32).indirect(list_t[:]))
+            return words
+
+        def product(acc, weight, block, moving):
+            cols = slice(block * P, (block + 1) * P)
+            nc.tensor.matmul_mx(
+                out=acc,
+                lhsT=weight[0][:, cols].bitcast(FP8X4),
+                lhsT_scale=weight[1][:, cols],
+                rhs=moving[0][:].bitcast(FP8X4),
+                rhs_scale=moving[1][:],
+                start=True,
+                stop=True,
+            )
+
+        xa_scales = pick_scales(offs_t, "xa_scales")
+        xb_scales = pick_scales(two_t, "xb_scales")
+        w1_q = quantise(cast_dealt(w1_raw, "w1_bf"), H, "w1")
+        xa_words = pick_words(offs_t, "xa_words")
+        y_rows = []
+        for t in range(PACK):
+            acc = bank(t, [P, S])
+            product(acc[:], w1_q, t, (xa_words, xa_scales))
+            y_t = keep.tile([P, S], F32, name=f"y{t}")
+            nc.scalar.copy(y_t[:], acc[:])
+            y_rows.append(y_t)
+        xb_words = pick_words(two_t, "xb_words")
+
+        def minus_difference(window, start, count, upper, dst):
+            return (
+                lambda: nc.vector.tensor_copy(upper, window[:].indirect(entries(hi_t, start, count))),
+                lambda: nc.vector.tensor_tensor(dst, window[:].indirect(entries(lo_t, start, count)), upper, ALU.subtract),
+            )
+
+        ndx, inv = [], []
+
+        def y_stage(t):
+            upper = keep.tile([P, S], F32, name=f"yhi{t}")
+            d = keep.tile([P, S], F32, name=f"ndx{t}")
+            steps = [
+                minus_difference(y_rows[t], a, HALF, upper[:, a : a + HALF], d[:, a : a + HALF])
+                for a in (0, HALF)
+            ]
+            for k in range(2):
+                for step in steps:
+                    step[k]()
+            ndx.append(d)
+
+        def inverse_stage(t):
+            sq = keep.tile([P, S], F32, name=f"sq{t}")
+            nc.scalar.activation(sq[:], ndx[t][:], ACT.Square)
+            root = keep.tile([P, S], F32, name=f"root{t}")
+            nc.scalar.activation(root[:], sq[:], ACT.Abs_reciprocal_sqrt, bias=0.25)
+            r = keep.tile([P, S], F32, name=f"inv{t}")
+            nc.scalar.activation(r[:], root[:], ACT.Square)
+            inv.append(r)
+
+        w2_bf = cast_dealt(w2_raw, "w2_bf")
+        y_stage(0)
+        y_stage(1)
+        w2_q = quantise(w2_bf, H, "w2")
+        inverse_stage(0)
+        c_rows = []
+        for t in range(PACK):
+            acc = bank(PACK + t, [P, S])
+            product(acc[:], w2_q, t, (xb_words, xb_scales))
+            c_t = keep.tile([P, S], F32, name=f"c{t}")
+            nc.scalar.activation(c_t[:], acc[:], ACT.Copy, scale=gain[:, t : t + 1])
+            c_rows.append(c_t)
+        y_stage(2)
+        y_stage(3)
+        for t in range(1, PACK):
+            inverse_stage(t)
+        w3_bf = cast_plain(w3_raw, "w3_bf")
+
+        out_rows = out.rearrange("(b p) j -> p b j", p=P)
+        slope = []
+        w3_q = []
+        for ci, (start, count) in enumerate(CHUNKS):
+            cols = slice(start, start + count)
+            upper = keep.tile([P, PACK, count], F32, name=f"chi{ci}", tag="chi")
+            ndy = keep.tile([P, PACK, count], F32, name=f"ndy{ci}", tag="ndy")
+            z = keep.tile([P, PACK, count], BF16, name=f"z{ci}")
+            for t0 in (0, 2):
+                steps = [
+                    minus_difference(c_rows[t], start, count, upper[:, t, :], ndy[:, t, :])
+                    for t in (t0, t0 + 1)
+                ]
+                for k in range(2):
+                    for step in steps:
+                        step[k]()
+            if ci == 0:
+                for t in range(PACK):
+                    q = keep.tile([P, S], F32, name=f"slope{t}")
+                    nc.vector.tensor_tensor(q[:], ndx[t][:], inv[t][:], ALU.mult)
+                    slope.append(q)
+            for t in range(PACK):
+                nc.vector.tensor_tensor(z[:, t, :], ndy[:, t, :], slope[t][:, cols], ALU.mult)
+            if ci == 0:
+                w3_q.append(quantise(w3_bf, N, "w3"))
+            grouped = keep.tile([P, count, PACK], BF16, name=f"zg{ci}", align_bytes=64)
+            weave = nc.vector.tensor_copy if ci == len(CHUNKS) - 1 else nc.scalar.copy
+            weave(
+                grouped[:].rearrange("p (c i) t -> p c t i", i=4),
+                z[:].rearrange("p t (c i) -> p c t i", i=4),
+            )
+            z_q = quantise(grouped[:].rearrange("p c t -> p (c t)"), count, f"z{ci}")
+            per_bank = 512 // count
+            for g in range(PACK // per_bank):
+                blocks = slice(g * per_bank, (g + 1) * per_bank)
+                acc = bank(2 * ci + g, [P, per_bank, count])
+                for b in range(per_bank):
+                    product(acc[:, b, :], w3_q[0], g * per_bank + b, z_q)
+                total = keep.tile([P, per_bank, count], F32, name=f"total{ci}_{g}")
+                nc.vector.tensor_tensor(total[:], acc[:], res_t[:, blocks, cols], ALU.add)
+                nc.sync.dma_start(out_rows[:, blocks, cols], total[:])

@@ -1,6 +1,7 @@
 from contextlib import ExitStack
 
 import concourse.mybir as mybir
+from concourse.masks import make_identity
 
 K, T, S, N, H = 512, 2048, 512, 512, 512
 FLOPS = 2 * K * H * S * 2 + 2 * H * N * S
@@ -19,7 +20,6 @@ P = 128
 PACK = 4
 LANES = 16
 HALF = S // 2
-CHUNKS = ((0, 256), (256, 128), (384, 128))
 
 
 def tile_picked_localslope_none_p_kernel(
@@ -30,6 +30,7 @@ def tile_picked_localslope_none_p_kernel(
     with ExitStack() as ctx:
         lists = ctx.enter_context(tc.tile_pool(name="lists", bufs=1))
         keep = ctx.enter_context(tc.tile_pool(name="keep", bufs=1))
+        ring = ctx.enter_context(tc.tile_pool(name="ring", bufs=3))
         psum = ctx.enter_context(tc.psum_pool(name="psum", bufs=1))
 
         def load_list(src, name):
@@ -54,6 +55,13 @@ def tile_picked_localslope_none_p_kernel(
 
         x_scale_table = keep.tile([P, T], U8, name="x_scale_table")
         nc.vector.memset(x_scale_table[:].bitcast(I32), 0)
+        y_rows = [keep.tile([P, 2 * S], F32, name=f"y{t}") for t in range(PACK)]
+        c_rows = [keep.tile([P, 2 * S if t < 2 else S], F32, name=f"c{t}") for t in range(PACK)]
+        for wide in y_rows + c_rows[:2]:
+            nc.vector.memset(wide[:, S:], 0.0)
+        identity = keep.tile([P, P], F32, name="identity")
+        nc.vector.memset(identity[:], 0.0)
+        make_identity(nc, identity[:], nomemset=True)
         scale_rows = x_scales[0].bitcast(I32)
         offs_t = load_list(offs, "offs_t")
         two_t = load_list(two, "two_t")
@@ -122,100 +130,134 @@ def tile_picked_localslope_none_p_kernel(
         xb_scales = pick_scales(two_t, "xb_scales")
         w1_q = quantise(cast_dealt(w1_raw, "w1_bf"), H, "w1")
         xa_words = pick_words(offs_t, "xa_words")
-        y_rows = []
         for t in range(PACK):
             acc = bank(t, [P, S])
             product(acc[:], w1_q, t, (xa_words, xa_scales))
-            y_t = keep.tile([P, S], F32, name=f"y{t}")
-            nc.scalar.copy(y_t[:], acc[:])
-            y_rows.append(y_t)
+            nc.scalar.copy(y_rows[t][:, :S], acc[:])
         xb_words = pick_words(two_t, "xb_words")
 
-        def minus_difference(window, start, count, upper, dst):
-            return (
-                lambda: nc.vector.tensor_copy(upper, window[:].indirect(entries(hi_t, start, count))),
-                lambda: nc.vector.tensor_tensor(dst, window[:].indirect(entries(lo_t, start, count)), upper, ALU.subtract),
+        def turned_differences(rows, t, halves, accs):
+            start, count = halves[0] * HALF, len(halves) * HALF
+            upper = ring.tile([P, count], F32, name="upper", tag="upper")
+            nc.vector.tensor_copy(upper[:], rows[t][:].indirect(entries(hi_t, start, count)))
+            lower = ring.tile([P, count], F32, name="lower", tag="lower")
+            nc.vector.tensor_scalar(
+                lower[:], rows[t][:].indirect(entries(lo_t, start, count)), -1.0, 0.0, ALU.mult, ALU.add
             )
+            for block in range(count // P):
+                cols = slice(block * P, (block + 1) * P)
+                dst = accs[block // 2][:, block % 2, t % 2, :]
+                nc.tensor.matmul(dst, upper[:, cols], identity[:], start=True, stop=False, is_transpose=True)
+                nc.tensor.matmul(dst, lower[:, cols], identity[:], start=False, stop=True, is_transpose=True)
 
-        ndx, inv = [], []
+        def paired(acc):
+            return acc[:].rearrange("j b e p -> j b p e")
 
-        def y_stage(t):
-            upper = keep.tile([P, S], F32, name=f"yhi{t}")
-            d = keep.tile([P, S], F32, name=f"ndx{t}")
-            steps = [
-                minus_difference(y_rows[t], a, HALF, upper[:, a : a + HALF], d[:, a : a + HALF])
-                for a in (0, HALF)
-            ]
-            for k in range(2):
-                for step in steps:
-                    step[k]()
-            ndx.append(d)
+        dx, inv = {}, {}
+        slope = {}
 
-        def inverse_stage(t):
-            sq = keep.tile([P, S], F32, name=f"sq{t}")
-            nc.scalar.activation(sq[:], ndx[t][:], ACT.Square)
-            root = keep.tile([P, S], F32, name=f"root{t}")
+        def x_stage(u):
+            accs = [bank(2 * u + h, [P, 2, 2, P]) for h in range(2)]
+            for t in (2 * u, 2 * u + 1):
+                turned_differences(y_rows, t, (0, 1), accs)
+            for h in range(2):
+                dx[h, u] = paired(accs[h])
+
+        def inverse_stage(h, u):
+            sq = keep.tile([P, 2, P, 2], F32, name=f"sq{h}{u}")
+            nc.scalar.activation(sq[:], dx[h, u], ACT.Square)
+            root = keep.tile([P, 2, P, 2], F32, name=f"root{h}{u}")
             nc.scalar.activation(root[:], sq[:], ACT.Abs_reciprocal_sqrt, bias=0.25)
-            r = keep.tile([P, S], F32, name=f"inv{t}")
+            r = keep.tile([P, 2, P, 2], F32, name=f"inv{h}{u}")
             nc.scalar.activation(r[:], root[:], ACT.Square)
-            inv.append(r)
+            inv[h, u] = r
+
+        def slope_stage(h, u):
+            q = keep.tile([P, 2, P, 2], F32, name=f"slope{h}{u}")
+            nc.vector.tensor_tensor(q[:], dx[h, u], inv[h, u][:], ALU.mult)
+            slope[h, u] = q
+
+        def z_stage(dy, factor, name):
+            z = keep.tile([P, 2, P, 2], BF16, name=name)
+            nc.vector.tensor_tensor(z[:], dy, factor, ALU.mult)
+            return z[:].rearrange("j s p e -> j (s p e)").bitcast(F32)
+
+        def turn_back(words, places):
+            for s, place in enumerate(places):
+                nc.tensor.transpose(place, words[:, s * P : (s + 1) * P], identity[:])
+
+        def weave(acc, blocks, name):
+            grouped = keep.tile([P, blocks * P * PACK], BF16, name=name, align_bytes=64)
+            nc.scalar.copy(
+                grouped[:].bitcast(F32).rearrange("p (b j u) -> p b j u", b=blocks, u=2),
+                acc[:].rearrange("p b u j -> p b j u"),
+            )
+            return grouped
+
+        out_rows = out.rearrange("(b p) j -> p b j", p=P)
+
+        def last_products(z_q, count, banks):
+            per_bank = 512 // count
+            accs = []
+            for g, b0 in enumerate(banks):
+                acc = bank(b0, [P, per_bank, count])
+                for b in range(per_bank):
+                    product(acc[:, b, :], w3_q, g * per_bank + b, z_q)
+                accs.append(acc)
+            return accs
+
+        def finish(accs, start, count):
+            per_bank = 512 // count
+            cols = slice(start, start + count)
+            for g, acc in enumerate(accs):
+                blocks = slice(g * per_bank, (g + 1) * per_bank)
+                total = keep.tile([P, per_bank, count], F32, name=f"total{start}_{g}")
+                nc.vector.tensor_tensor(total[:], acc[:], res_t[:, blocks, cols], ALU.add)
+                nc.sync.dma_start(out_rows[:, blocks, cols], total[:])
 
         w2_bf = cast_dealt(w2_raw, "w2_bf")
-        y_stage(0)
-        y_stage(1)
+        x_stage(0)
         w2_q = quantise(w2_bf, H, "w2")
-        inverse_stage(0)
-        c_rows = []
+        inverse_stage(0, 0)
         for t in range(PACK):
             acc = bank(PACK + t, [P, S])
             product(acc[:], w2_q, t, (xb_words, xb_scales))
-            c_t = keep.tile([P, S], F32, name=f"c{t}")
-            nc.scalar.activation(c_t[:], acc[:], ACT.Copy, scale=gain[:, t : t + 1])
-            c_rows.append(c_t)
-        y_stage(2)
-        y_stage(3)
-        for t in range(1, PACK):
-            inverse_stage(t)
+            nc.scalar.activation(c_rows[t][:, :S], acc[:], ACT.Copy, scale=gain[:, t : t + 1])
+        x_stage(1)
+        inverse_stage(1, 0)
+        inverse_stage(0, 1)
+        inverse_stage(1, 1)
         w3_bf = cast_plain(w3_raw, "w3_bf")
 
-        out_rows = out.rearrange("(b p) j -> p b j", p=P)
-        slope = []
-        w3_q = []
-        for ci, (start, count) in enumerate(CHUNKS):
-            cols = slice(start, start + count)
-            upper = keep.tile([P, PACK, count], F32, name=f"chi{ci}", tag="chi")
-            ndy = keep.tile([P, PACK, count], F32, name=f"ndy{ci}", tag="ndy")
-            z = keep.tile([P, PACK, count], BF16, name=f"z{ci}")
-            for t0 in (0, 2):
-                steps = [
-                    minus_difference(c_rows[t], start, count, upper[:, t, :], ndy[:, t, :])
-                    for t in (t0, t0 + 1)
-                ]
-                for k in range(2):
-                    for step in steps:
-                        step[k]()
-            if ci == 0:
-                for t in range(PACK):
-                    q = keep.tile([P, S], F32, name=f"slope{t}")
-                    nc.vector.tensor_tensor(q[:], ndx[t][:], inv[t][:], ALU.mult)
-                    slope.append(q)
-            for t in range(PACK):
-                nc.vector.tensor_tensor(z[:, t, :], ndy[:, t, :], slope[t][:, cols], ALU.mult)
-            if ci == 0:
-                w3_q.append(quantise(w3_bf, N, "w3"))
-            grouped = keep.tile([P, count, PACK], BF16, name=f"zg{ci}", align_bytes=64)
-            weave = nc.vector.tensor_copy if ci == len(CHUNKS) - 1 else nc.scalar.copy
-            weave(
-                grouped[:].rearrange("p (c i) t -> p c t i", i=4),
-                z[:].rearrange("p t (c i) -> p c t i", i=4),
-            )
-            z_q = quantise(grouped[:].rearrange("p c t -> p (c t)"), count, f"z{ci}")
-            per_bank = 512 // count
-            for g in range(PACK // per_bank):
-                blocks = slice(g * per_bank, (g + 1) * per_bank)
-                acc = bank(2 * ci + g, [P, per_bank, count])
-                for b in range(per_bank):
-                    product(acc[:, b, :], w3_q[0], g * per_bank + b, z_q)
-                total = keep.tile([P, per_bank, count], F32, name=f"total{ci}_{g}")
-                nc.vector.tensor_tensor(total[:], acc[:], res_t[:, blocks, cols], ALU.add)
-                nc.sync.dma_start(out_rows[:, blocks, cols], total[:])
+        back = {}
+
+        def z_and_back(h, u, acc):
+            if u == 0:
+                back[h] = bank(h, [P, 2, 2, P])
+            words = z_stage(paired(acc), slope[h, u][:], f"z{h}{u}")
+            turn_back(words, [back[h][:, b, u, :] for b in range(2)])
+
+        dy0 = [bank(4 + h, [P, 2, 2, P]) for h in range(2)]
+        turned_differences(c_rows, 0, (0, 1), dy0)
+        turned_differences(c_rows, 1, (0, 1), dy0)
+        slope_stage(0, 0)
+        slope_stage(1, 0)
+        dy01 = bank(6, [P, 2, 2, P])
+        turned_differences(c_rows, 2, (0,), [dy01])
+        z_and_back(0, 0, dy0[0])
+        z_and_back(1, 0, dy0[1])
+        turned_differences(c_rows, 3, (0,), [dy01])
+        slope_stage(0, 1)
+        slope_stage(1, 1)
+        w3_q = quantise(w3_bf, N, "w3")
+        z_and_back(0, 1, dy01)
+        grouped0 = weave(back[0], 2, "zg0")
+        dy11 = bank(7, [P, 2, 2, P])
+        turned_differences(c_rows, 2, (1,), [dy11])
+        turned_differences(c_rows, 3, (1,), [dy11])
+        sums0 = last_products(quantise(grouped0[:], HALF, "z0"), HALF, (2, 3))
+        z_and_back(1, 1, dy11)
+        grouped1 = weave(back[1], 2, "zg1")
+        finish(sums0, 0, HALF)
+        sums1 = last_products(quantise(grouped1[:], HALF, "z1"), HALF, (4, 5))
+        finish(sums1, HALF, HALF)

@@ -40,7 +40,7 @@ def tile_picked_localslope_none_p_kernel(
 
         def load_weight_half(w, name, h):
             rows = w.rearrange("(p j) c -> p j c", j=PACK)
-            raw = keep.tile([P, PACK, H // 2], F32, name=f"{name}_raw{h}")
+            raw = keep.tile([P, PACK, H // 2], F32, name=f"{name}_raw{h}", tag=f"{name}_raw{h}")
             nc.sync.dma_start(raw[:], rows[:, :, h * (H // 2) : (h + 1) * (H // 2)])
             return raw
 
@@ -56,8 +56,12 @@ def tile_picked_localslope_none_p_kernel(
         x_scale_table = keep.tile([P, T], U8, name="x_scale_table")
         nc.vector.memset(x_scale_table[:].bitcast(I32), 0)
         y_rows = [keep.tile([P, 2 * S], F32, name=f"y{t}") for t in range(PACK)]
-        c_rows = [keep.tile([P, 2 * S if t < 2 else S], F32, name=f"c{t}") for t in range(PACK)]
-        for wide in y_rows + c_rows[:2]:
+        c_minus = [
+            keep.tile([P, 2 * S if t < 2 else S], F32, name=f"c_minus{t}", tag=f"c_minus{t}", align_bytes=64)
+            for t in range(PACK)
+        ]
+        y_hi = [wide[:, S:] for wide in c_minus[:2]]
+        for wide in y_rows:
             nc.vector.memset(wide[:, S:], 0.0)
         identity = keep.tile([P, P], F32, name="identity")
         nc.vector.memset(identity[:], 0.0)
@@ -81,7 +85,7 @@ def tile_picked_localslope_none_p_kernel(
         nc.sync.dma_start(res_t[:], res.rearrange("(b p) j -> p b j", p=P))
 
         def cast_dealt(halves, name):
-            grouped = keep.tile([P, PACK, P, PACK], BF16, name=name, align_bytes=64)
+            grouped = keep.tile([P, PACK, P, PACK], BF16, name=name, tag=name, align_bytes=64)
             for h, raw in enumerate(halves):
                 nc.scalar.copy(
                     grouped[:, :, h * 64 : (h + 1) * 64, :].rearrange("p t m j -> p m j t"),
@@ -98,8 +102,8 @@ def tile_picked_localslope_none_p_kernel(
                 )
             return grouped[:].rearrange("p c j -> p (c j)")
 
-        def quantise(values, width, name):
-            words = keep.tile([P, width], U32, name=f"{name}_words", align_bytes=64)
+        def quantise(values, width, name, held=None):
+            words = keep.tile([P, width], U32, name=f"{name}_words", tag=held or f"{name}_words", align_bytes=64)
             scales = keep.tile([P, width], U8, name=f"{name}_scales", align_bytes=64)
             nc.vector.quantize_mx(out=words[:].bitcast(FP8X4), scales=scales[:], in_=values)
             return words, scales
@@ -109,77 +113,96 @@ def tile_picked_localslope_none_p_kernel(
             nc.vector.tensor_copy(scales[:], x_scale_table[:].indirect(list_t[:]))
             return scales
 
-        def pick_words(list_t, name):
-            words = keep.tile([P, S], U32, name=name, align_bytes=64)
-            nc.vector.tensor_copy(words[:], x_word_table[:].bitcast(U32).indirect(list_t[:]))
+        def pick_words(list_t, name, pieces):
+            words = keep.tile([P, S], U32, name=name, tag=name, align_bytes=64)
+            count = S // pieces
+            for start in range(0, S, count):
+                nc.vector.tensor_copy(
+                    words[:, start : start + count],
+                    x_word_table[:].bitcast(U32).indirect(entries(list_t, start, count)),
+                )
             return words
 
-        def product(acc, weight, block, moving):
+        def product(acc, weight, block, moving, places=slice(None)):
             cols = slice(block * P, (block + 1) * P)
             nc.tensor.matmul_mx(
                 out=acc,
                 lhsT=weight[0][:, cols].bitcast(FP8X4),
                 lhsT_scale=weight[1][:, cols],
-                rhs=moving[0][:].bitcast(FP8X4),
-                rhs_scale=moving[1][:],
+                rhs=moving[0][:, places].bitcast(FP8X4),
+                rhs_scale=moving[1][:, places],
                 start=True,
                 stop=True,
             )
 
+        warm = keep.tile([P, 1], F32, name="warm")
+        nc.scalar.activation(warm[:], y_rows[0][:, S : S + 1], ACT.Abs_reciprocal_sqrt, bias=0.25)
+
         xa_scales = pick_scales(offs_t, "xa_scales")
         xb_scales = pick_scales(two_t, "xb_scales")
         w1_q = quantise(cast_dealt(w1_raw, "w1_bf"), H, "w1")
-        xa_words = pick_words(offs_t, "xa_words")
-        for t in range(PACK):
-            acc = bank(t, [P, S])
-            product(acc[:], w1_q, t, (xa_words, xa_scales))
-            nc.scalar.copy(y_rows[t][:, :S], acc[:])
-        xb_words = pick_words(two_t, "xb_words")
+        xa_words = pick_words(offs_t, "xa_words", 2)
+        y_sums = [bank(t, [P, S]) for t in range(PACK)]
+        for h in range(2):
+            places = slice(h * HALF, (h + 1) * HALF)
+            product(y_sums[0][:, places], w1_q, 0, (xa_words, xa_scales), places)
+        for t in range(1, PACK):
+            product(y_sums[t][:], w1_q, t, (xa_words, xa_scales))
+        xb_words = pick_words(two_t, "xb_words", 1)
 
-        def turned_differences(rows, t, halves, accs):
-            start, count = halves[0] * HALF, len(halves) * HALF
-            upper = ring.tile([P, count], F32, name="upper", tag="upper")
-            nc.vector.tensor_copy(upper[:], rows[t][:].indirect(entries(hi_t, start, count)))
+        def y_out(t):
+            nc.scalar.copy(y_rows[t][:, :S], y_sums[t][:])
+
+        def paired(acc):
+            return acc.rearrange("j s e p -> j s p e")
+
+        ndx = [
+            keep.tile([P, S], F32, name=f"ndx{t}", tag="xa_words" if t == 0 else f"ndx{t}", align_bytes=64)
+            for t in range(PACK)
+        ]
+        dx_turned, inv = {}, {}
+
+        def fetch_hi(t):
+            nc.vector.tensor_copy(y_hi[t], y_rows[t][:].indirect(hi_t[:]))
+
+        def fetch_lo(t):
+            nc.vector.tensor_tensor(ndx[t][:], y_rows[t][:].indirect(lo_t[:]), y_hi[t], ALU.subtract)
+            u, e = divmod(t, 2)
+            for block in range(PACK):
+                h, b = divmod(block, 2)
+                if (h, u) not in dx_turned:
+                    dx_turned[h, u] = bank(2 * u + h, [P, 2, 2, P])
+                nc.tensor.transpose(dx_turned[h, u][:, b, e, :], ndx[t][:, block * P : (block + 1) * P], identity[:])
+
+        def inverse_stage(u):
+            sq = keep.tile([P, PACK, P, 2], F32, name=f"sq{u}", tag="w3_raw1")
+            for h in range(2):
+                nc.scalar.activation(sq[:, 2 * h : 2 * h + 2], paired(dx_turned[h, u][:]), ACT.Square)
+            root = keep.tile([P, PACK, P, 2], F32, name=f"root{u}")
+            nc.scalar.activation(root[:], sq[:], ACT.Abs_reciprocal_sqrt, bias=0.25)
+            for h in range(2):
+                inv[h, u] = keep.tile([P, 2, P, 2], F32, name=f"inv{h}{u}", tag=f"inv{h}{u}")
+                nc.scalar.activation(inv[h, u][:], root[:, 2 * h : 2 * h + 2], ACT.Square)
+
+        def turned_products(t, first, places, held=None):
+            start, count = first * P, len(places) * P
+            factor = ndx[t][:, start : start + count]
+            if held is None:
+                upper = ring.tile([P, count], F32, name="upper", tag="upper")
+            else:
+                upper = keep.tile([P, count], F32, name="upper", tag=held)
+            nc.vector.tensor_tensor(upper[:], c_minus[t][:].indirect(entries(hi_t, start, count)), factor, ALU.mult)
             lower = ring.tile([P, count], F32, name="lower", tag="lower")
-            nc.vector.tensor_scalar(
-                lower[:], rows[t][:].indirect(entries(lo_t, start, count)), -1.0, 0.0, ALU.mult, ALU.add
-            )
-            for block in range(count // P):
+            nc.vector.tensor_tensor(lower[:], c_plus[t][:].indirect(entries(lo_t, start, count)), factor, ALU.mult)
+            for block, place in enumerate(places):
                 cols = slice(block * P, (block + 1) * P)
-                dst = accs[block // 2][:, block % 2, t % 2, :]
+                dst = place[:, t % 2, :]
                 nc.tensor.matmul(dst, upper[:, cols], identity[:], start=True, stop=False, is_transpose=True)
                 nc.tensor.matmul(dst, lower[:, cols], identity[:], start=False, stop=True, is_transpose=True)
 
-        def paired(acc):
-            return acc[:].rearrange("j b e p -> j b p e")
-
-        dx, inv = {}, {}
-        slope = {}
-
-        def x_stage(u):
-            accs = [bank(2 * u + h, [P, 2, 2, P]) for h in range(2)]
-            for t in (2 * u, 2 * u + 1):
-                turned_differences(y_rows, t, (0, 1), accs)
-            for h in range(2):
-                dx[h, u] = paired(accs[h])
-
-        def inverse_stage(h, u):
-            sq = keep.tile([P, 2, P, 2], F32, name=f"sq{h}{u}")
-            nc.scalar.activation(sq[:], dx[h, u], ACT.Square)
-            root = keep.tile([P, 2, P, 2], F32, name=f"root{h}{u}")
-            nc.scalar.activation(root[:], sq[:], ACT.Abs_reciprocal_sqrt, bias=0.25)
-            r = keep.tile([P, 2, P, 2], F32, name=f"inv{h}{u}")
-            nc.scalar.activation(r[:], root[:], ACT.Square)
-            inv[h, u] = r
-
-        def slope_stage(h, u):
-            q = keep.tile([P, 2, P, 2], F32, name=f"slope{h}{u}")
-            nc.vector.tensor_tensor(q[:], dx[h, u], inv[h, u][:], ALU.mult)
-            slope[h, u] = q
-
-        def z_stage(dy, factor, name):
-            z = keep.tile([P, 2, P, 2], BF16, name=name)
-            nc.vector.tensor_tensor(z[:], dy, factor, ALU.mult)
+        def z_stage(acc, factor, slots, name):
+            z = keep.tile([P, slots, P, 2], BF16, name=name)
+            nc.vector.tensor_tensor(z[:], paired(acc[:]), factor, ALU.mult)
             return z[:].rearrange("j s p e -> j (s p e)").bitcast(F32)
 
         def turn_back(words, places):
@@ -215,49 +238,67 @@ def tile_picked_localslope_none_p_kernel(
                 nc.vector.tensor_tensor(total[:], acc[:], res_t[:, blocks, cols], ALU.add)
                 nc.sync.dma_start(out_rows[:, blocks, cols], total[:])
 
+        y_out(0)
+        y_out(1)
         w2_bf = cast_dealt(w2_raw, "w2_bf")
-        x_stage(0)
+        y_out(2)
+        y_out(3)
+        minus_gain = keep.tile([P, PACK], F32, name="minus_gain")
+        nc.gpsimd.tensor_scalar(minus_gain[:], gain[:], -1.0, 0.0, ALU.mult, ALU.add)
+        fetch_hi(0)
+        fetch_hi(1)
+        fetch_lo(0)
+        fetch_lo(1)
         w2_q = quantise(w2_bf, H, "w2")
-        inverse_stage(0, 0)
+        c_sums = [bank(PACK + t, [P, S]) for t in range(PACK)]
         for t in range(PACK):
-            acc = bank(PACK + t, [P, S])
-            product(acc[:], w2_q, t, (xb_words, xb_scales))
-            nc.scalar.activation(c_rows[t][:, :S], acc[:], ACT.Copy, scale=gain[:, t : t + 1])
-        x_stage(1)
-        inverse_stage(1, 0)
-        inverse_stage(0, 1)
-        inverse_stage(1, 1)
+            product(c_sums[t][:], w2_q, t, (xb_words, xb_scales))
+
+        def c_out(t):
+            nc.scalar.activation(c_minus[t][:, :S], c_sums[t][:], ACT.Copy, scale=minus_gain[:, t : t + 1])
+            nc.scalar.activation(c_plus[t][:, :S], c_sums[t][:], ACT.Copy, scale=gain[:, t : t + 1])
+
+        c_plus = [
+            keep.tile([P, 2 * S], F32, name="c_plus0", tag="w2_bf", align_bytes=64),
+            keep.tile([P, 2 * S], F32, name="c_plus1", tag="w2_raw1"),
+            keep.tile([P, S], F32, name="c_plus2"),
+            keep.tile([P, S], F32, name="c_plus3"),
+        ]
+        y_hi.extend(wide[:, S:] for wide in c_plus[:2])
+        fetch_hi(2)
+        fetch_hi(3)
+        fetch_lo(2)
+        fetch_lo(3)
         w3_bf = cast_plain(w3_raw, "w3_bf")
+        for u in range(2):
+            c_out(2 * u)
+            c_out(2 * u + 1)
+            inverse_stage(u)
 
-        back = {}
-
-        def z_and_back(h, u, acc):
-            if u == 0:
-                back[h] = bank(h, [P, 2, 2, P])
-            words = z_stage(paired(acc), slope[h, u][:], f"z{h}{u}")
-            turn_back(words, [back[h][:, b, u, :] for b in range(2)])
-
-        dy0 = [bank(4 + h, [P, 2, 2, P]) for h in range(2)]
-        turned_differences(c_rows, 0, (0, 1), dy0)
-        turned_differences(c_rows, 1, (0, 1), dy0)
-        slope_stage(0, 0)
-        slope_stage(1, 0)
-        dy01 = bank(6, [P, 2, 2, P])
-        turned_differences(c_rows, 2, (0,), [dy01])
-        z_and_back(0, 0, dy0[0])
-        z_and_back(1, 0, dy0[1])
-        turned_differences(c_rows, 3, (0,), [dy01])
-        slope_stage(0, 1)
-        slope_stage(1, 1)
-        w3_q = quantise(w3_bf, N, "w3")
-        z_and_back(0, 1, dy01)
-        grouped0 = weave(back[0], 2, "zg0")
-        dy11 = bank(7, [P, 2, 2, P])
-        turned_differences(c_rows, 2, (1,), [dy11])
-        turned_differences(c_rows, 3, (1,), [dy11])
-        sums0 = last_products(quantise(grouped0[:], HALF, "z0"), HALF, (2, 3))
-        z_and_back(1, 1, dy11)
-        grouped1 = weave(back[1], 2, "zg1")
-        finish(sums0, 0, HALF)
-        sums1 = last_products(quantise(grouped1[:], HALF, "z1"), HALF, (4, 5))
-        finish(sums1, HALF, HALF)
+        pa, pb = bank(4, [P, 2, 2, P]), bank(5, [P, 2, 2, P])
+        for t in (0, 1):
+            turned_products(t, 0, [pa[:, 0], pa[:, 1], pb[:, 0], pb[:, 1]])
+        pc, pd = bank(6, [P, 2, 2, P]), bank(7, [P, 1, 2, P])
+        back_a, back_b = bank(0, [P, 2, 2, P]), bank(1, [P, 1, 2, P])
+        turned_products(2, 0, [pc[:, 0], pc[:, 1], pd[:, 0]])
+        turn_back(z_stage(pa, inv[0, 0][:], 2, "za"), [back_a[:, 0, 0, :], back_a[:, 1, 0, :]])
+        zb = z_stage(pb, inv[1, 0][:], 2, "zb")
+        back_c = bank(5, [P, 1, 2, P])
+        turn_back(zb, [back_b[:, 0, 0, :], back_c[:, 0, 0, :]])
+        turned_products(3, 0, [pc[:, 0], pc[:, 1], pd[:, 0]])
+        pe = bank(4, [P, 1, 2, P])
+        turned_products(2, 3, [pe[:, 0]])
+        turn_back(z_stage(pc, inv[0, 1][:], 2, "zc"), [back_a[:, 0, 1, :], back_a[:, 1, 1, :]])
+        grouped_a = weave(back_a, 2, "zga")
+        turn_back(z_stage(pd, inv[1, 1][:, 0:1], 1, "zd"), [back_b[:, 0, 1, :]])
+        grouped_b = weave(back_b, 1, "zgb")
+        turned_products(3, 3, [pe[:, 0]], "inv01")
+        w3_q = quantise(w3_bf, N, "w3", "c_minus3")
+        turn_back(z_stage(pe, inv[1, 1][:, 1:2], 1, "ze"), [back_c[:, 0, 1, :]])
+        grouped_c = weave(back_c, 1, "zgc")
+        sums_a = last_products(quantise(grouped_a[:], 256, "za"), 256, (2, 3))
+        sums_b = last_products(quantise(grouped_b[:], 128, "zb"), 128, (6,))
+        sums_c = last_products(quantise(grouped_c[:], 128, "zc"), 128, (7,))
+        finish(sums_a, 0, 256)
+        finish(sums_b, 256, 128)
+        finish(sums_c, 384, 128)

from contextlib import ExitStack

import concourse.mybir as mybir
from concourse.masks import make_identity

K, T, S, N, H = 512, 2048, 512, 512, 512
FLOPS = 2 * K * H * S * 2 + 2 * H * N * S

F32 = mybir.dt.float32
BF16 = mybir.dt.bfloat16
I32 = mybir.dt.int32
U32 = mybir.dt.uint32
U16 = mybir.dt.uint16
U8 = mybir.dt.uint8
FP8X4 = mybir.dt.float8_e4m3fn_x4
ACT = mybir.ActivationFunctionType
ALU = mybir.AluOpType

P = 128
PACK = 4
LANES = 16
HALF = S // 2


def tile_picked_localslope_none_p_kernel(
    tc, x_words, x_scales, w1, w2, gn, w3, res, offs, two, hi, lo, out
):
    nc = tc.nc

    with ExitStack() as ctx:
        lists = ctx.enter_context(tc.tile_pool(name="lists", bufs=1))
        keep = ctx.enter_context(tc.tile_pool(name="keep", bufs=1))
        ring = ctx.enter_context(tc.tile_pool(name="ring", bufs=3))
        psum = ctx.enter_context(tc.psum_pool(name="psum", bufs=1))

        def load_list(src, name):
            tile = lists.tile([P, S // LANES], U16, name=name)
            nc.sync.dma_start(tile[:], src)
            return tile

        def load_weight_half(w, name, h):
            rows = w.rearrange("(p j) c -> p j c", j=PACK)
            raw = keep.tile([P, PACK, H // 2], F32, name=f"{name}_raw{h}", tag=f"{name}_raw{h}")
            nc.sync.dma_start(raw[:], rows[:, :, h * (H // 2) : (h + 1) * (H // 2)])
            return raw

        def load_weight_halves(w, name):
            return [load_weight_half(w, name, h) for h in range(2)]

        def entries(tile, start, count):
            return tile[:, start // LANES : (start + count) // LANES]

        def bank(b, shape):
            return psum.tile(shape, F32, name=f"bank{b}", tag=f"bank{b}")

        x_scale_table = keep.tile([P, T], U8, name="x_scale_table")
        nc.vector.memset(x_scale_table[:].bitcast(I32), 0)
        y_rows = [keep.tile([P, 2 * S], F32, name=f"y{t}") for t in range(PACK)]
        c_minus = [
            keep.tile([P, 2 * S if t < 2 else S], F32, name=f"c_minus{t}", tag=f"c_minus{t}", align_bytes=64)
            for t in range(PACK)
        ]
        y_hi = [wide[:, S:] for wide in c_minus[:2]]
        for wide in y_rows:
            nc.vector.memset(wide[:, S:], 0.0)
        identity = keep.tile([P, P], F32, name="identity")
        nc.vector.memset(identity[:], 0.0)
        make_identity(nc, identity[:], nomemset=True)
        scale_rows = x_scales[0].bitcast(I32)
        offs_t = load_list(offs, "offs_t")
        two_t = load_list(two, "two_t")
        w1_raw = [load_weight_half(w1, "w1", 0)]
        for r in range(PACK):
            nc.sync.dma_start(x_scale_table[r:P:32, :].bitcast(I32), scale_rows[r:16:PACK, :])
        w1_raw.append(load_weight_half(w1, "w1", 1))
        x_word_table = keep.tile([P, T], I32, name="x_word_table")
        nc.sync.dma_start(x_word_table[:], x_words[0].rearrange("p n t -> p (n t)").bitcast(I32))
        hi_t = load_list(hi, "hi_t")
        lo_t = load_list(lo, "lo_t")
        w2_raw = load_weight_halves(w2, "w2")
        gain = keep.tile([P, PACK], F32, name="gain")
        nc.sync.dma_start(gain[:], gn.rearrange("(p t) o -> p (t o)", t=PACK))
        w3_raw = load_weight_halves(w3, "w3")
        res_t = keep.tile([P, PACK, S], F32, name="res_t")
        nc.sync.dma_start(res_t[:], res.rearrange("(b p) j -> p b j", p=P))

        def cast_dealt(halves, name):
            grouped = keep.tile([P, PACK, P, PACK], BF16, name=name, tag=name, align_bytes=64)
            for h, raw in enumerate(halves):
                nc.scalar.copy(
                    grouped[:, :, h * 64 : (h + 1) * 64, :].rearrange("p t m j -> p m j t"),
                    raw[:].rearrange("p j (m t) -> p m j t", t=PACK),
                )
            return grouped[:].rearrange("p t m j -> p (t m j)")

        def cast_plain(halves, name):
            grouped = keep.tile([P, N, PACK], BF16, name=name, align_bytes=64)
            for h, raw in enumerate(halves):
                nc.scalar.copy(
                    grouped[:, h * 256 : (h + 1) * 256, :].rearrange("p (c i) j -> p c j i", i=4),
                    raw[:].rearrange("p j (c i) -> p c j i", i=4),
                )
            return grouped[:].rearrange("p c j -> p (c j)")

        def quantise(values, width, name, held=None):
            words = keep.tile([P, width], U32, name=f"{name}_words", tag=held or f"{name}_words", align_bytes=64)
            scales = keep.tile([P, width], U8, name=f"{name}_scales", align_bytes=64)
            nc.vector.quantize_mx(out=words[:].bitcast(FP8X4), scales=scales[:], in_=values)
            return words, scales

        def pick_scales(list_t, name):
            scales = keep.tile([P, S], U8, name=name, align_bytes=64)
            nc.vector.tensor_copy(scales[:], x_scale_table[:].indirect(list_t[:]))
            return scales

        def pick_words(list_t, name, pieces):
            words = keep.tile([P, S], U32, name=name, tag=name, align_bytes=64)
            count = S // pieces
            for start in range(0, S, count):
                nc.vector.tensor_copy(
                    words[:, start : start + count],
                    x_word_table[:].bitcast(U32).indirect(entries(list_t, start, count)),
                )
            return words

        def product(acc, weight, block, moving, places=slice(None)):
            cols = slice(block * P, (block + 1) * P)
            nc.tensor.matmul_mx(
                out=acc,
                lhsT=weight[0][:, cols].bitcast(FP8X4),
                lhsT_scale=weight[1][:, cols],
                rhs=moving[0][:, places].bitcast(FP8X4),
                rhs_scale=moving[1][:, places],
                start=True,
                stop=True,
            )

        warm = keep.tile([P, 1], F32, name="warm")
        nc.scalar.activation(warm[:], y_rows[0][:, S : S + 1], ACT.Abs_reciprocal_sqrt, bias=0.25)

        xa_scales = pick_scales(offs_t, "xa_scales")
        xb_scales = pick_scales(two_t, "xb_scales")
        w1_q = quantise(cast_dealt(w1_raw, "w1_bf"), H, "w1")
        xa_words = pick_words(offs_t, "xa_words", 2)
        y_sums = [bank(t, [P, S]) for t in range(PACK)]
        for h in range(2):
            places = slice(h * HALF, (h + 1) * HALF)
            product(y_sums[0][:, places], w1_q, 0, (xa_words, xa_scales), places)
        for t in range(1, PACK):
            product(y_sums[t][:], w1_q, t, (xa_words, xa_scales))
        xb_words = pick_words(two_t, "xb_words", 1)

        def y_out(t):
            nc.scalar.copy(y_rows[t][:, :S], y_sums[t][:])

        def paired(acc):
            return acc.rearrange("j s e p -> j s p e")

        ndx = [
            keep.tile([P, S], F32, name=f"ndx{t}", tag="xa_words" if t == 0 else f"ndx{t}", align_bytes=64)
            for t in range(PACK)
        ]
        dx_turned, inv = {}, {}

        def fetch_hi(t):
            nc.vector.tensor_copy(y_hi[t], y_rows[t][:].indirect(hi_t[:]))

        def fetch_lo(t):
            nc.vector.tensor_tensor(ndx[t][:], y_rows[t][:].indirect(lo_t[:]), y_hi[t], ALU.subtract)
            u, e = divmod(t, 2)
            for block in range(PACK):
                h, b = divmod(block, 2)
                if (h, u) not in dx_turned:
                    dx_turned[h, u] = bank(2 * u + h, [P, 2, 2, P])
                nc.tensor.transpose(dx_turned[h, u][:, b, e, :], ndx[t][:, block * P : (block + 1) * P], identity[:])

        def inverse_stage(u):
            sq = keep.tile([P, PACK, P, 2], F32, name=f"sq{u}", tag="w3_raw1")
            for h in range(2):
                nc.scalar.activation(sq[:, 2 * h : 2 * h + 2], paired(dx_turned[h, u][:]), ACT.Square)
            root = keep.tile([P, PACK, P, 2], F32, name=f"root{u}")
            nc.scalar.activation(root[:], sq[:], ACT.Abs_reciprocal_sqrt, bias=0.25)
            for h in range(2):
                inv[h, u] = keep.tile([P, 2, P, 2], F32, name=f"inv{h}{u}", tag=f"inv{h}{u}")
                nc.scalar.activation(inv[h, u][:], root[:, 2 * h : 2 * h + 2], ACT.Square)

        def turned_products(t, first, places, held=None):
            start, count = first * P, len(places) * P
            factor = ndx[t][:, start : start + count]
            if held is None:
                upper = ring.tile([P, count], F32, name="upper", tag="upper")
            else:
                upper = keep.tile([P, count], F32, name="upper", tag=held)
            nc.vector.tensor_tensor(upper[:], c_minus[t][:].indirect(entries(hi_t, start, count)), factor, ALU.mult)
            lower = ring.tile([P, count], F32, name="lower", tag="lower")
            nc.vector.tensor_tensor(lower[:], c_plus[t][:].indirect(entries(lo_t, start, count)), factor, ALU.mult)
            for block, place in enumerate(places):
                cols = slice(block * P, (block + 1) * P)
                dst = place[:, t % 2, :]
                nc.tensor.matmul(dst, upper[:, cols], identity[:], start=True, stop=False, is_transpose=True)
                nc.tensor.matmul(dst, lower[:, cols], identity[:], start=False, stop=True, is_transpose=True)

        def z_stage(acc, factor, slots, name):
            z = keep.tile([P, slots, P, 2], BF16, name=name)
            nc.vector.tensor_tensor(z[:], paired(acc[:]), factor, ALU.mult)
            return z[:].rearrange("j s p e -> j (s p e)").bitcast(F32)

        def turn_back(words, places):
            for s, place in enumerate(places):
                nc.tensor.transpose(place, words[:, s * P : (s + 1) * P], identity[:])

        def weave(acc, blocks, name):
            grouped = keep.tile([P, blocks * P * PACK], BF16, name=name, align_bytes=64)
            nc.scalar.copy(
                grouped[:].bitcast(F32).rearrange("p (b j u) -> p b j u", b=blocks, u=2),
                acc[:].rearrange("p b u j -> p b j u"),
            )
            return grouped

        out_rows = out.rearrange("(b p) j -> p b j", p=P)

        def last_products(z_q, count, banks):
            per_bank = 512 // count
            accs = []
            for g, b0 in enumerate(banks):
                acc = bank(b0, [P, per_bank, count])
                for b in range(per_bank):
                    product(acc[:, b, :], w3_q, g * per_bank + b, z_q)
                accs.append(acc)
            return accs

        def finish(accs, start, count):
            per_bank = 512 // count
            cols = slice(start, start + count)
            for g, acc in enumerate(accs):
                blocks = slice(g * per_bank, (g + 1) * per_bank)
                total = keep.tile([P, per_bank, count], F32, name=f"total{start}_{g}")
                nc.vector.tensor_tensor(total[:], acc[:], res_t[:, blocks, cols], ALU.add)
                nc.sync.dma_start(out_rows[:, blocks, cols], total[:])

        y_out(0)
        y_out(1)
        w2_bf = cast_dealt(w2_raw, "w2_bf")
        y_out(2)
        y_out(3)
        minus_gain = keep.tile([P, PACK], F32, name="minus_gain")
        nc.gpsimd.tensor_scalar(minus_gain[:], gain[:], -1.0, 0.0, ALU.mult, ALU.add)
        fetch_hi(0)
        fetch_hi(1)
        fetch_lo(0)
        fetch_lo(1)
        w2_q = quantise(w2_bf, H, "w2")
        c_sums = [bank(PACK + t, [P, S]) for t in range(PACK)]
        for t in range(PACK):
            product(c_sums[t][:], w2_q, t, (xb_words, xb_scales))

        def c_out(t):
            nc.scalar.activation(c_minus[t][:, :S], c_sums[t][:], ACT.Copy, scale=minus_gain[:, t : t + 1])
            nc.scalar.activation(c_plus[t][:, :S], c_sums[t][:], ACT.Copy, scale=gain[:, t : t + 1])

        c_plus = [
            keep.tile([P, 2 * S], F32, name="c_plus0", tag="w2_bf", align_bytes=64),
            keep.tile([P, 2 * S], F32, name="c_plus1", tag="w2_raw1"),
            keep.tile([P, S], F32, name="c_plus2"),
            keep.tile([P, S], F32, name="c_plus3"),
        ]
        y_hi.extend(wide[:, S:] for wide in c_plus[:2])
        fetch_hi(2)
        fetch_hi(3)
        fetch_lo(2)
        fetch_lo(3)
        w3_bf = cast_plain(w3_raw, "w3_bf")
        for u in range(2):
            c_out(2 * u)
            c_out(2 * u + 1)
            inverse_stage(u)

        pa, pb = bank(4, [P, 2, 2, P]), bank(5, [P, 2, 2, P])
        for t in (0, 1):
            turned_products(t, 0, [pa[:, 0], pa[:, 1], pb[:, 0], pb[:, 1]])
        pc, pd = bank(6, [P, 2, 2, P]), bank(7, [P, 1, 2, P])
        back_a, back_b = bank(0, [P, 2, 2, P]), bank(1, [P, 1, 2, P])
        turned_products(2, 0, [pc[:, 0], pc[:, 1], pd[:, 0]])
        turn_back(z_stage(pa, inv[0, 0][:], 2, "za"), [back_a[:, 0, 0, :], back_a[:, 1, 0, :]])
        zb = z_stage(pb, inv[1, 0][:], 2, "zb")
        back_c = bank(5, [P, 1, 2, P])
        turn_back(zb, [back_b[:, 0, 0, :], back_c[:, 0, 0, :]])
        turned_products(3, 0, [pc[:, 0], pc[:, 1], pd[:, 0]])
        pe = bank(4, [P, 1, 2, P])
        turned_products(2, 3, [pe[:, 0]])
        turn_back(z_stage(pc, inv[0, 1][:], 2, "zc"), [back_a[:, 0, 1, :], back_a[:, 1, 1, :]])
        grouped_a = weave(back_a, 2, "zga")
        turn_back(z_stage(pd, inv[1, 1][:, 0:1], 1, "zd"), [back_b[:, 0, 1, :]])
        grouped_b = weave(back_b, 1, "zgb")
        turned_products(3, 3, [pe[:, 0]], "inv01")
        w3_q = quantise(w3_bf, N, "w3", "c_minus3")
        turn_back(z_stage(pe, inv[1, 1][:, 1:2], 1, "ze"), [back_c[:, 0, 1, :]])
        grouped_c = weave(back_c, 1, "zgc")
        sums_a = last_products(quantise(grouped_a[:], 256, "za"), 256, (2, 3))
        sums_b = last_products(quantise(grouped_b[:], 128, "zb"), 128, (6,))
        sums_c = last_products(quantise(grouped_c[:], 128, "zc"), 128, (7,))
        finish(sums_a, 0, 256)
        finish(sums_b, 256, 128)
        finish(sums_c, 384, 128)
